import numpy as np
import ml_dtypes


def mxq(x, axis, fmt="e4m3"):
    dtype, down = {"e4m3": (ml_dtypes.float8_e4m3fn, 7), "e5m2": (ml_dtypes.float8_e5m2, 14)}[fmt]
    v = np.moveaxis(np.asarray(x, np.float32).astype(ml_dtypes.bfloat16).astype(np.float64), axis, -1)
    blocks = v.reshape(v.shape[:-1] + (-1, 32))
    amax = np.abs(blocks).max(-1, keepdims=True)
    byte = np.maximum(np.where(amax > 0, np.frexp(amax)[1] - 1 + 127, 0) - down, 1)
    scale = np.exp2(byte - 127.0)
    codes = (blocks / scale).astype(np.float32).astype(dtype).astype(np.float64)
    return np.moveaxis((codes * scale).reshape(v.shape), -1, axis)


WIDE = False


def mx_kscale(k):
    if not WIDE:
        return np.ones(k)
    levels = np.array([10, -10, 5, -5, 0])
    if k % 512:
        return np.exp2(np.random.permutation(np.resize(levels, k // 32))).repeat(32)
    a = np.empty((k // 512, 16))
    for p in range(k // 512):
        a[p, :8] = np.random.permutation(np.resize(levels, 8))
        for g in range(8):
            far = levels[np.abs(levels - a[p, g]) >= 10]
            a[p, g + 8] = far[np.random.randint(len(far))]
    return np.exp2(a.ravel()).repeat(32)


def f64(x):
    return np.asarray(x).astype(np.float64)


def striped(idx):
    return np.tile(np.asarray(idx).reshape(-1, 16).T, (8, 1)).astype(np.uint16)


def unstriped(offs):
    return offs[:16].T.reshape(-1).astype(np.int64)


def striped8(idx):
    return np.asarray(idx).reshape(8, -1, 16).transpose(0, 2, 1).reshape(128, -1).astype(np.uint16)


def unstriped8(offs):
    return offs.reshape(8, 16, -1).transpose(0, 2, 1).reshape(8, -1).astype(np.int64)


def pick8(x, idx, run):
    r = np.arange(len(x))
    return x[r[:, None], idx[r % (8 * run) // run]]


E2M1 = np.array([0.0, 0.5, 1.0, 1.5, 2.0, 3.0, 4.0, 6.0, -0.0, -0.5, -1.0, -1.5, -2.0, -3.0, -4.0, -6.0])


def pack_weight(w, fmt):
    k, n = w.shape
    w = f64(np.asarray(w, np.float32).astype(ml_dtypes.bfloat16)).reshape(k // 32, 32, n)
    amax = np.abs(w).max(1)
    if fmt == "e4m3":
        byte = np.frexp(amax)[1] - 1 + 127 - 7
    else:
        mant, ex = np.frexp(amax / 6.0)
        byte = np.where(mant > 0.5, ex, ex - 1) + 127
    byte = np.clip(np.where(amax > 0, byte, 1), 1, 254)
    scaled = (w * np.exp2(127.0 - byte)[:, None, :]).reshape(k, n).astype(np.float32)
    by_word = np.ascontiguousarray(scaled.reshape(k // 512, 128, 4, n).transpose(0, 1, 3, 2))
    if fmt == "e4m3":
        words = by_word.astype(ml_dtypes.float8_e4m3fn).view(np.uint8)
    else:
        c = by_word.astype(ml_dtypes.float4_e2m1fn).view(np.uint8) & 0xF
        words = (c[..., 0::2] | (c[..., 1::2] << 4)).reshape(k // 512, 128, 2 * n)
    return np.ascontiguousarray(words), np.ascontiguousarray(byte.astype(np.uint8).reshape(k // 512, 16, n))


def unpack_weight(words, scales, fmt):
    g, _, n = scales.shape
    words = np.ascontiguousarray(words).reshape(g, 128, n, -1)
    if fmt == "e4m3":
        vals = words.view(ml_dtypes.float8_e4m3fn).astype(np.float64)
    else:
        nib = np.empty((g, 128, n, 4), np.uint8)
        nib[..., 0::2] = words & 0xF
        nib[..., 1::2] = words >> 4
        vals = E2M1[nib]
    vals = vals * np.repeat(np.exp2(scales.astype(np.float64) - 127.0), 8, axis=1)[..., None]
    return vals.transpose(0, 1, 3, 2).reshape(g * 512, n)


def bf(x):
    return np.asarray(x, np.float32).astype(ml_dtypes.bfloat16)


def planes(Y):
    r, m = Y.shape
    b = f64(bf(Y)).reshape(r // 32, 32, m)
    amax = np.abs(b).max(1)
    byte = np.clip(np.where(amax > 0, np.frexp(amax)[1] - 1 + 127 - 7, 1), 1, 254)
    codes = (b * np.exp2(127.0 - byte)[:, None, :]).reshape(r, m).astype(np.float32).astype(ml_dtypes.float8_e4m3fn).view(np.uint8)
    words = codes.reshape(r // 512, 128, 4, m).transpose(0, 1, 3, 2)
    return np.ascontiguousarray(words), np.ascontiguousarray(byte.astype(np.uint8).reshape(r // 512, 16, m))


D, T, I, G, U, Q = 512, 2048, 1024, 128, 512, 512


def setup_inputs():
    n = np.random.standard_normal
    idx = np.stack([np.random.permutation(T)[:I] for _ in range(8)])
    idx2 = np.random.permutation(U)[:G]
    fd = mx_kscale(D)
    piecep = pack_weight(n((D, T)) / fd[:, None], "e4m3")
    return {
        "query": (n((D, Q)) * 1.0 / np.sqrt(D) * fd[:, None]).astype(np.float32),
        "piece_words": piecep[0],
        "piece_scales": piecep[1],
        "prior": (0.5 * n((Q, U))).astype(np.float32),
        "offs": striped8(idx),
        "offs2": striped(idx2),
    }


def reference(query, piece_words, piece_scales, prior, offs, offs2):
    idx = unstriped8(offs)
    idx2 = unstriped(offs2)
    pieceu = unpack_weight(piece_words, piece_scales, "e4m3")
    queryq = mxq(f64(query), 0, "e4m3")
    pieceidxg = pick8(pieceu, idx, 64)
    a = queryq.T @ pieceidxg
    s = np.log(np.exp(a).reshape(Q, G, I // G).mean(axis=2)) + f64(prior)[:, idx2]
    p = np.exp(s - np.max(s, axis=1, keepdims=True))
    y = p / np.sum(p, axis=1, keepdims=True) * 64.0
    words, scales = planes(y)
    return y, words, scales

@@ -1,0 +1,202 @@
+from contextlib import ExitStack
+
+import concourse.mybir as mybir
+from concourse.masks import make_identity
+
+D, T, I, G, U, Q = 512, 2048, 1024, 128, 512, 512
+FLOPS = 2 * D * Q * I
+
+F32 = mybir.dt.float32
+BF16 = mybir.dt.bfloat16
+I32 = mybir.dt.int32
+U32 = mybir.dt.uint32
+U16 = mybir.dt.uint16
+U8 = mybir.dt.uint8
+FP8X4 = mybir.dt.float8_e4m3fn_x4
+ALU = mybir.AluOpType
+ACT = mybir.ActivationFunctionType
+X = mybir.AxisListType.X
+
+P = 128
+PACK = 4
+PAGE = I // G
+HALF = 512
+HALVES = I // HALF
+HALF_PAGES = HALF // PAGE
+Q_CHUNKS = 2
+SCALE_ROW = 14
+
+
+def tile_attend_composedpages_pl_kernel(tc, query, piece_words, piece_scales, prior, offs, offs2, out_0, out_1, out_2):
+    nc = tc.nc
+    with ExitStack() as ctx:
+        lists = ctx.enter_context(tc.tile_pool(name="lists", bufs=1))
+        keep = ctx.enter_context(tc.tile_pool(name="keep", bufs=1))
+        score_banks = ctx.enter_context(tc.psum_pool(name="score_banks", bufs=6))
+        turn_banks = ctx.enter_context(tc.psum_pool(name="turn_banks", bufs=1))
+
+        piece_list = lists.tile([P, I // 16], U16, name="piece_list")
+        page_list = lists.tile([P, G // 16], U16, name="page_list")
+        nc.sync.dma_start(piece_list[:], offs)
+
+        scale_store = keep.tile([P, T], U8, name="scale_store")
+        nc.vector.memset(scale_store[:].bitcast(I32), 0)
+        for quad in range(4):
+            first = 32 * quad + SCALE_ROW
+            nc.sync.dma_start(
+                scale_store[first : first + 4, :].bitcast(I32),
+                piece_scales[0, 4 * quad : 4 * quad + 4, :].bitcast(I32),
+            )
+        word_store = keep.tile([P, T], U32, name="word_store")
+        nc.sync.dma_start(word_store[:].bitcast(I32), piece_words[0].rearrange("p n t -> p (n t)").bitcast(I32))
+
+        chunk = Q // Q_CHUNKS
+        query_rows = query.rearrange("(p t) q -> p t q", t=PACK)
+        query_raw = []
+        for c in range(Q_CHUNKS):
+            raw = keep.tile([P, PACK, chunk], F32, name="query_raw%d" % c)
+            nc.sync.dma_start(raw[:], query_rows[:, :, c * chunk : (c + 1) * chunk])
+            query_raw.append(raw)
+
+        nc.sync.dma_start(page_list[:], offs2)
+        prior_rows = prior.rearrange("(p r) u -> p r u", r=PACK)
+        prior_table = []
+        for r in range(PACK):
+            table = keep.tile([P, U], F32, name="prior_table%d" % r)
+            nc.sync.dma_start(table[:], prior_rows[:, r, :])
+            prior_table.append(table)
+
+        identity = keep.tile([P, P], F32, name="identity")
+        make_identity(nc, identity[:])
+        key_scales = keep.tile([P, I], U8, name="key_scales", align_bytes=64)
+        nc.gpsimd.memset(key_scales[:].bitcast(I32), 0)
+
+        picked_scales = keep.tile([P, I], U8, name="picked_scales")
+        nc.vector.tensor_copy(picked_scales[:], scale_store[:].indirect(piece_list[:]))
+        for quad in range(4):
+            first = 32 * quad + SCALE_ROW
+            nc.scalar.dma_start(
+                key_scales[32 * quad : 32 * quad + 4, :].bitcast(I32),
+                picked_scales[first : first + 4, :].bitcast(I32),
+            )
+
+        key_words = []
+        for h in range(HALVES):
+            picked = keep.tile([P, HALF], U32, name="key_words%d" % h, align_bytes=64)
+            nc.vector.tensor_copy(picked[:], word_store[:].indirect(piece_list[:, h * HALF // 16 : (h + 1) * HALF // 16]))
+            key_words.append(picked)
+
+        query_bf = keep.tile([P, PACK, P, PACK], BF16, name="query_bf", align_bytes=64)
+        for c in range(Q_CHUNKS):
+            ms = slice(c * chunk // PACK, (c + 1) * chunk // PACK)
+            nc.scalar.activation(
+                query_bf[:, :, ms, :].rearrange("p r m t -> p m t r"),
+                query_raw[c][:].rearrange("p t (m r) -> p m t r", r=PACK),
+                ACT.Copy,
+            )
+        query_words = keep.tile([P, PACK, P], U32, name="query_words", align_bytes=64)
+        query_scales = keep.tile([P, PACK, P], U8, name="query_scales", align_bytes=64)
+        for r in range(PACK):
+            nc.vector.quantize_mx(
+                out=query_words[:, r, :].bitcast(FP8X4),
+                scales=query_scales[:, r, :],
+                in_=query_bf[:, r, :, :].rearrange("p m t -> p (m t)"),
+            )
+
+        picked_prior = keep.tile([P, PACK, G], F32, name="picked_prior")
+        for r in range(PACK):
+            nc.scalar.activation(picked_prior[:, r, :], prior_table[r][:].indirect(page_list[:]), ACT.Copy)
+        neg_prior_max = keep.tile([P, PACK], F32, name="neg_prior_max")
+
+        y = keep.tile([P, PACK, G], F32, name="y")
+        last = PACK - 1
+        for r in range(PACK):
+            neg_max = keep.tile([P, HALVES], F32, name="neg_max%d" % r)
+            slot_exp = keep.tile([P, I], F32, name="slot_exp%d" % r)
+            for h in range(HALVES):
+                scores = score_banks.tile([P, HALF], F32, name="scores")
+                nc.tensor.matmul_mx(
+                    out=scores[:],
+                    lhsT=query_words[:, r, :].bitcast(FP8X4),
+                    lhsT_scale=query_scales[:, r, :],
+                    rhs=key_words[h][:].bitcast(FP8X4),
+                    rhs_scale=key_scales[:, h * HALF : (h + 1) * HALF],
+                    start=True,
+                    stop=True,
+                )
+                nc.vector.tensor_reduce(neg_max[:, h : h + 1], scores[:], X, ALU.max, negate=True)
+                pages = slice(h * HALF_PAGES, (h + 1) * HALF_PAGES)
+                if r == last:
+                    nc.scalar.activation(
+                        slot_exp[:, h * HALF : (h + 1) * HALF], scores[:], ACT.Exp, bias=neg_max[:, h : h + 1]
+                    )
+                else:
+                    nc.scalar.activation(
+                        slot_exp[:].rearrange("p (j g) -> p j g", j=PAGE)[:, :, pages],
+                        scores[:].rearrange("p (g j) -> p j g", j=PAGE),
+                        ACT.Exp,
+                        bias=neg_max[:, h : h + 1],
+                    )
+            if r == 0:
+                nc.vector.tensor_reduce(neg_prior_max[:], picked_prior[:], X, ALU.max, negate=True)
+
+            neg_shift = keep.tile([P, 1], F32, name="neg_shift%d" % r)
+            nc.gpsimd.tensor_scalar(
+                neg_shift[:], neg_max[:, 0:1], neg_max[:, 1:2], neg_prior_max[:, r : r + 1], ALU.min, ALU.add
+            )
+            page_bias = keep.tile([P, HALVES], F32, name="page_bias%d" % r)
+            nc.gpsimd.tensor_scalar(page_bias[:], neg_max[:], -1.0, neg_shift[:], ALU.mult, ALU.add)
+            page_weight = keep.tile([P, G], F32, name="page_weight%d" % r)
+            for h in range(HALVES):
+                pages = slice(h * HALF_PAGES, (h + 1) * HALF_PAGES)
+                nc.scalar.activation(page_weight[:, pages], picked_prior[:, r, pages], ACT.Exp, bias=page_bias[:, h : h + 1])
+
+            if r == last:
+                page_sum = keep.tile([P, G], F32, name="page_sum")
+                for h in range(HALVES):
+                    pages = slice(h * HALF_PAGES, (h + 1) * HALF_PAGES)
+                    nc.vector.tensor_reduce(
+                        page_sum[:, pages],
+                        slot_exp[:, h * HALF : (h + 1) * HALF].rearrange("p (g j) -> p g j", j=PAGE),
+                        X,
+                        ALU.add,
+                    )
+            else:
+                turned_sum = turn_banks.tile([P, P], F32, name="turned_sum")
+                for j in range(PAGE):
+                    nc.tensor.matmul(
+                        turned_sum[:],
+                        lhsT=slot_exp[:, j * G : (j + 1) * G],
+                        rhs=identity[:],
+                        start=(j == 0),
+                        stop=(j == PAGE - 1),
+                        is_transpose=True,
+                    )
+                turned_copy = keep.tile([P, P], F32, name="turned_copy%d" % r)
+                nc.scalar.copy(turned_copy[:], turned_sum[:])
+                page_sum = turn_banks.tile([P, G], F32, name="page_sum_bank")
+                nc.tensor.transpose(page_sum[:], turned_copy[:], identity[:])
+
+            weighted = keep.tile([P, G], F32, name="weighted%d" % r)
+            row_sum = keep.tile([P, 1], F32, name="row_sum%d" % r)
+            nc.vector.scalar_tensor_tensor(
+                weighted[:], page_sum[:], 1.0, page_weight[:], ALU.mult, ALU.mult, accum_out=row_sum[:]
+            )
+            inverse = keep.tile([P, 1], F32, name="inverse%d" % r)
+            nc.vector.reciprocal(inverse[:], row_sum[:])
+            nc.vector.tensor_scalar(y[:, r, :], weighted[:], inverse[:], 64.0, ALU.mult, ALU.mult)
+
+        nc.sync.dma_start(out_0.rearrange("(p r) g -> p r g", r=PACK), y[:])
+
+        y_bf = keep.tile([P, G, PACK], BF16, name="y_bf", align_bytes=64)
+        nc.vector.tensor_copy(y_bf[:], y[:].rearrange("p r g -> p g r"))
+        y_words = keep.tile([P, G], U32, name="y_words", align_bytes=64)
+        y_scales = keep.tile([P, G], U8, name="y_scales", align_bytes=64)
+        nc.vector.quantize_mx(out=y_words[:].bitcast(FP8X4), scales=y_scales[:], in_=y_bf[:].rearrange("p g r -> p (g r)"))
+        nc.sync.dma_start(out_1[0].rearrange("p g r -> p (g r)").bitcast(I32), y_words[:].bitcast(I32))
+        for quad in range(4):
+            queue = nc.scalar if quad % 2 == 0 else nc.sync
+            queue.dma_start(
+                out_2[0, 4 * quad : 4 * quad + 4, :].bitcast(I32),
+                y_scales[32 * quad : 32 * quad + 4, :].bitcast(I32),
+            )

@@ -23,8 +23,9 @@ PAGE = I // G
 HALF = 512
 HALVES = I // HALF
 HALF_PAGES = HALF // PAGE
-Q_CHUNKS = 2
-SCALE_ROW = 14
+Q_CHUNKS = (128, 128, 128, 128)
+BLOCK_PARTS = 8
+PAIRS = (slice(0, 2), slice(2, 4))
 
 
 def tile_attend_composedpages_pl_kernel(tc, query, piece_words, piece_scales, prior, offs, offs2, out_0, out_1, out_2):
@@ -33,52 +34,44 @@ def tile_attend_composedpages_pl_kernel(tc, query, piece_words, piece_scales, pr
         lists = ctx.enter_context(tc.tile_pool(name="lists", bufs=1))
         keep = ctx.enter_context(tc.tile_pool(name="keep", bufs=1))
         score_banks = ctx.enter_context(tc.psum_pool(name="score_banks", bufs=6))
-        turn_banks = ctx.enter_context(tc.psum_pool(name="turn_banks", bufs=1))
+        turn_banks = ctx.enter_context(tc.psum_pool(name="turn_banks", bufs=2))
 
         piece_list = lists.tile([P, I // 16], U16, name="piece_list")
         page_list = lists.tile([P, G // 16], U16, name="page_list")
         nc.sync.dma_start(piece_list[:], offs)
+        nc.sync.dma_start(page_list[:], offs2)
 
-        scale_store = keep.tile([P, T], U8, name="scale_store")
+        scale_store = keep.tile([P, T], U8, name="scale_store", tag="scales_then_prior")
         nc.vector.memset(scale_store[:].bitcast(I32), 0)
-        for quad in range(4):
-            first = 32 * quad + SCALE_ROW
-            nc.sync.dma_start(
-                scale_store[first : first + 4, :].bitcast(I32),
-                piece_scales[0, 4 * quad : 4 * quad + 4, :].bitcast(I32),
-            )
-        word_store = keep.tile([P, T], U32, name="word_store")
-        nc.sync.dma_start(word_store[:].bitcast(I32), piece_words[0].rearrange("p n t -> p (n t)").bitcast(I32))
-
-        chunk = Q // Q_CHUNKS
+        nc.sync.dma_start(scale_store[0:P:BLOCK_PARTS, :].bitcast(I32), piece_scales[0].bitcast(I32))
         query_rows = query.rearrange("(p t) q -> p t q", t=PACK)
         query_raw = []
-        for c in range(Q_CHUNKS):
+        first = 0
+        for c, chunk in enumerate(Q_CHUNKS):
             raw = keep.tile([P, PACK, chunk], F32, name="query_raw%d" % c)
-            nc.sync.dma_start(raw[:], query_rows[:, :, c * chunk : (c + 1) * chunk])
-            query_raw.append(raw)
-
-        nc.sync.dma_start(page_list[:], offs2)
-        prior_rows = prior.rearrange("(p r) u -> p r u", r=PACK)
-        prior_table = []
-        for r in range(PACK):
-            table = keep.tile([P, U], F32, name="prior_table%d" % r)
-            nc.sync.dma_start(table[:], prior_rows[:, r, :])
-            prior_table.append(table)
+            nc.sync.dma_start(raw[:], query_rows[:, :, first : first + chunk])
+            query_raw.append((raw, slice(first // PACK, (first + chunk) // PACK)))
+            first += chunk
+            if c == 0:
+                word_store = keep.tile([P, T], U32, name="word_store")
+                nc.sync.dma_start(word_store[:].bitcast(I32), piece_words[0].rearrange("p n t -> p (n t)").bitcast(I32))
 
         identity = keep.tile([P, P], F32, name="identity")
         make_identity(nc, identity[:])
         key_scales = keep.tile([P, I], U8, name="key_scales", align_bytes=64)
-        nc.gpsimd.memset(key_scales[:].bitcast(I32), 0)
+        nc.vector.memset(key_scales[:].bitcast(I32), 0)
 
         picked_scales = keep.tile([P, I], U8, name="picked_scales")
         nc.vector.tensor_copy(picked_scales[:], scale_store[:].indirect(piece_list[:]))
         for quad in range(4):
-            first = 32 * quad + SCALE_ROW
-            nc.scalar.dma_start(
+            nc.sync.dma_start(
                 key_scales[32 * quad : 32 * quad + 4, :].bitcast(I32),
-                picked_scales[first : first + 4, :].bitcast(I32),
+                picked_scales[32 * quad : 32 * quad + 32 : BLOCK_PARTS, :].bitcast(I32),
             )
+        prior_rows = prior.rearrange("(p r) u -> p r u", r=PACK)
+        prior_table = keep.tile([P, PACK, U], F32, name="prior_table", tag="scales_then_prior")
+        for r in range(PACK):
+            nc.sync.dma_start(prior_table[:, r, :], prior_rows[:, r, :])
 
         key_words = []
         for h in range(HALVES):
@@ -87,38 +80,39 @@ def tile_attend_composedpages_pl_kernel(tc, query, piece_words, piece_scales, pr
             key_words.append(picked)
 
         query_bf = keep.tile([P, PACK, P, PACK], BF16, name="query_bf", align_bytes=64)
-        for c in range(Q_CHUNKS):
-            ms = slice(c * chunk // PACK, (c + 1) * chunk // PACK)
+        for raw, ms in query_raw:
             nc.scalar.activation(
                 query_bf[:, :, ms, :].rearrange("p r m t -> p m t r"),
-                query_raw[c][:].rearrange("p t (m r) -> p m t r", r=PACK),
+                raw[:].rearrange("p t (m r) -> p m t r", r=PACK),
                 ACT.Copy,
             )
-        query_words = keep.tile([P, PACK, P], U32, name="query_words", align_bytes=64)
-        query_scales = keep.tile([P, PACK, P], U8, name="query_scales", align_bytes=64)
+        query_words, query_scales = [], []
         for r in range(PACK):
+            query_words.append(keep.tile([P, P], U32, name="query_words%d" % r, align_bytes=64))
+            query_scales.append(keep.tile([P, P], U8, name="query_scales%d" % r, align_bytes=64))
             nc.vector.quantize_mx(
-                out=query_words[:, r, :].bitcast(FP8X4),
-                scales=query_scales[:, r, :],
+                out=query_words[r][:].bitcast(FP8X4),
+                scales=query_scales[r][:],
                 in_=query_bf[:, r, :, :].rearrange("p m t -> p (m t)"),
             )
 
+        last = PACK - 1
         picked_prior = keep.tile([P, PACK, G], F32, name="picked_prior")
-        for r in range(PACK):
-            nc.scalar.activation(picked_prior[:, r, :], prior_table[r][:].indirect(page_list[:]), ACT.Copy)
+        for r in range(last):
+            nc.scalar.activation(picked_prior[:, r, :], prior_table[:, r, :].indirect(page_list[:]), ACT.Copy)
         neg_prior_max = keep.tile([P, PACK], F32, name="neg_prior_max")
 
         y = keep.tile([P, PACK, G], F32, name="y")
-        last = PACK - 1
+        slot_exps, neg_maxes = [], []
         for r in range(PACK):
             neg_max = keep.tile([P, HALVES], F32, name="neg_max%d" % r)
             slot_exp = keep.tile([P, I], F32, name="slot_exp%d" % r)
             for h in range(HALVES):
-                scores = score_banks.tile([P, HALF], F32, name="scores")
+                scores = score_banks.tile([P, HALF], F32, name="scores", tag="scores")
                 nc.tensor.matmul_mx(
                     out=scores[:],
-                    lhsT=query_words[:, r, :].bitcast(FP8X4),
-                    lhsT_scale=query_scales[:, r, :],
+                    lhsT=query_words[r][:].bitcast(FP8X4),
+                    lhsT_scale=query_scales[r][:],
                     rhs=key_words[h][:].bitcast(FP8X4),
                     rhs_scale=key_scales[:, h * HALF : (h + 1) * HALF],
                     start=True,
@@ -137,20 +131,24 @@ def tile_attend_composedpages_pl_kernel(tc, query, piece_words, piece_scales, pr
                         ACT.Exp,
                         bias=neg_max[:, h : h + 1],
                     )
-            if r == 0:
-                nc.vector.tensor_reduce(neg_prior_max[:], picked_prior[:], X, ALU.max, negate=True)
+            slot_exps.append(slot_exp)
+            neg_maxes.append(neg_max)
+            if r == 1:
+                nc.vector.tensor_copy(picked_prior[:, last, :], prior_table[:, last, :].indirect(page_list[:]))
+            if r < 2:
+                nc.vector.tensor_reduce(neg_prior_max[:, PAIRS[r]], picked_prior[:, PAIRS[r], :], X, ALU.max, negate=True)
 
+        for r in range(PACK):
+            slot_exp, neg_max = slot_exps[r], neg_maxes[r]
+            small = nc.vector if r == last else nc.gpsimd
             neg_shift = keep.tile([P, 1], F32, name="neg_shift%d" % r)
-            nc.gpsimd.tensor_scalar(
-                neg_shift[:], neg_max[:, 0:1], neg_max[:, 1:2], neg_prior_max[:, r : r + 1], ALU.min, ALU.add
-            )
+            small.tensor_scalar(neg_shift[:], neg_max[:, 0:1], neg_max[:, 1:2], neg_prior_max[:, r : r + 1], ALU.min, ALU.add)
             page_bias = keep.tile([P, HALVES], F32, name="page_bias%d" % r)
-            nc.gpsimd.tensor_scalar(page_bias[:], neg_max[:], -1.0, neg_shift[:], ALU.mult, ALU.add)
+            small.tensor_scalar(page_bias[:], neg_max[:], -1.0, neg_shift[:], ALU.mult, ALU.add)
             page_weight = keep.tile([P, G], F32, name="page_weight%d" % r)
             for h in range(HALVES):
                 pages = slice(h * HALF_PAGES, (h + 1) * HALF_PAGES)
                 nc.scalar.activation(page_weight[:, pages], picked_prior[:, r, pages], ACT.Exp, bias=page_bias[:, h : h + 1])
-
             if r == last:
                 page_sum = keep.tile([P, G], F32, name="page_sum")
                 for h in range(HALVES):
@@ -172,9 +170,9 @@ def tile_attend_composedpages_pl_kernel(tc, query, piece_words, piece_scales, pr
                         stop=(j == PAGE - 1),
                         is_transpose=True,
                     )
-                turned_copy = keep.tile([P, P], F32, name="turned_copy%d" % r)
+                turned_copy = keep.tile([P, P], F32, name="turned_copy%d" % r, align_bytes=64, tag="turned_copy%d" % r)
                 nc.scalar.copy(turned_copy[:], turned_sum[:])
-                page_sum = turn_banks.tile([P, G], F32, name="page_sum_bank")
+                page_sum = score_banks.tile([P, G], F32, name="page_sum_bank", tag="scores")
                 nc.tensor.transpose(page_sum[:], turned_copy[:], identity[:])
 
             weighted = keep.tile([P, G], F32, name="weighted%d" % r)
@@ -184,12 +182,15 @@ def tile_attend_composedpages_pl_kernel(tc, query, piece_words, piece_scales, pr
             )
             inverse = keep.tile([P, 1], F32, name="inverse%d" % r)
             nc.vector.reciprocal(inverse[:], row_sum[:])
-            nc.vector.tensor_scalar(y[:, r, :], weighted[:], inverse[:], 64.0, ALU.mult, ALU.mult)
+            if r == 2:
+                y_bf = keep.tile([P, G, PACK], BF16, name="y_bf", align_bytes=64, tag="turned_copy2")
+                nc.scalar.activation(y_bf[:, :, PAIRS[0]], y[:, PAIRS[0], :].rearrange("p r g -> p g r"), ACT.Copy)
+            if r >= 2:
+                nc.vector.tensor_scalar(y_bf[:, :, r], weighted[:], inverse[:], 64.0, ALU.mult, ALU.mult)
+            small.tensor_scalar(y[:, r, :], weighted[:], inverse[:], 64.0, ALU.mult, ALU.mult)
 
         nc.sync.dma_start(out_0.rearrange("(p r) g -> p r g", r=PACK), y[:])
 
-        y_bf = keep.tile([P, G, PACK], BF16, name="y_bf", align_bytes=64)
-        nc.vector.tensor_copy(y_bf[:], y[:].rearrange("p r g -> p g r"))
         y_words = keep.tile([P, G], U32, name="y_words", align_bytes=64)
         y_scales = keep.tile([P, G], U8, name="y_scales", align_bytes=64)
         nc.vector.quantize_mx(out=y_words[:].bitcast(FP8X4), scales=y_scales[:], in_=y_bf[:].rearrange("p g r -> p (g r)"))

@@ -126,8 +126,8 @@ def tile_attend_composedpages_pl_kernel(tc, query, piece_words, piece_scales, pr
                     )
                 else:
                     nc.scalar.activation(
-                        slot_exp[:].rearrange("p (j g) -> p j g", j=PAGE)[:, :, pages],
-                        scores[:].rearrange("p (g j) -> p j g", j=PAGE),
+                        slot_exp[:].rearrange("p (k e g) -> p k g e", e=2, g=G)[:, :, pages, :],
+                        scores[:].rearrange("p (g k e) -> p k g e", e=2, k=PAGE // 2),
                         ACT.Exp,
                         bias=neg_max[:, h : h + 1],
                     )
@@ -187,9 +187,11 @@ def tile_attend_composedpages_pl_kernel(tc, query, piece_words, piece_scales, pr
                 nc.scalar.activation(y_bf[:, :, PAIRS[0]], y[:, PAIRS[0], :].rearrange("p r g -> p g r"), ACT.Copy)
             if r >= 2:
                 nc.vector.tensor_scalar(y_bf[:, :, r], weighted[:], inverse[:], 64.0, ALU.mult, ALU.mult)
-            small.tensor_scalar(y[:, r, :], weighted[:], inverse[:], 64.0, ALU.mult, ALU.mult)
-
-        nc.sync.dma_start(out_0.rearrange("(p r) g -> p r g", r=PACK), y[:])
+            scaler = nc.vector if r >= 2 else nc.gpsimd
+            scaler.tensor_scalar(y[:, r, :], weighted[:], inverse[:], 64.0, ALU.mult, ALU.mult)
+            if r % 2 == 1:
+                pair = PAIRS[r // 2]
+                nc.sync.dma_start(out_0.rearrange("(p r) g -> p r g", r=PACK)[:, pair, :], y[:, pair, :])
 
         y_words = keep.tile([P, G], U32, name="y_words", align_bytes=64)
         y_scales = keep.tile([P, G], U8, name="y_scales", align_bytes=64)

@@ -82,8 +82,8 @@ def tile_attend_composedpages_pl_kernel(tc, query, piece_words, piece_scales, pr
         query_bf = keep.tile([P, PACK, P, PACK], BF16, name="query_bf", align_bytes=64)
         for raw, ms in query_raw:
             nc.scalar.activation(
-                query_bf[:, :, ms, :].rearrange("p r m t -> p m t r"),
-                raw[:].rearrange("p t (m r) -> p m t r", r=PACK),
+                query_bf[:, :, ms, :].rearrange("p r m t -> p m r t"),
+                raw[:].rearrange("p t (m r) -> p m r t", r=PACK),
                 ACT.Copy,
             )
         query_words, query_scales = [], []

from contextlib import ExitStack

import concourse.mybir as mybir
from concourse.masks import make_identity

D, T, I, G, U, Q = 512, 2048, 1024, 128, 512, 512
FLOPS = 2 * D * Q * I

F32 = mybir.dt.float32
BF16 = mybir.dt.bfloat16
I32 = mybir.dt.int32
U32 = mybir.dt.uint32
U16 = mybir.dt.uint16
U8 = mybir.dt.uint8
FP8X4 = mybir.dt.float8_e4m3fn_x4
ALU = mybir.AluOpType
ACT = mybir.ActivationFunctionType
X = mybir.AxisListType.X

P = 128
PACK = 4
PAGE = I // G
HALF = 512
HALVES = I // HALF
HALF_PAGES = HALF // PAGE
Q_CHUNKS = (128, 128, 128, 128)
BLOCK_PARTS = 8
PAIRS = (slice(0, 2), slice(2, 4))


def tile_attend_composedpages_pl_kernel(tc, query, piece_words, piece_scales, prior, offs, offs2, out_0, out_1, out_2):
    nc = tc.nc
    with ExitStack() as ctx:
        lists = ctx.enter_context(tc.tile_pool(name="lists", bufs=1))
        keep = ctx.enter_context(tc.tile_pool(name="keep", bufs=1))
        score_banks = ctx.enter_context(tc.psum_pool(name="score_banks", bufs=6))
        turn_banks = ctx.enter_context(tc.psum_pool(name="turn_banks", bufs=2))

        piece_list = lists.tile([P, I // 16], U16, name="piece_list")
        page_list = lists.tile([P, G // 16], U16, name="page_list")
        nc.sync.dma_start(piece_list[:], offs)
        nc.sync.dma_start(page_list[:], offs2)

        scale_store = keep.tile([P, T], U8, name="scale_store", tag="scales_then_prior")
        nc.vector.memset(scale_store[:].bitcast(I32), 0)
        nc.sync.dma_start(scale_store[0:P:BLOCK_PARTS, :].bitcast(I32), piece_scales[0].bitcast(I32))
        query_rows = query.rearrange("(p t) q -> p t q", t=PACK)
        query_raw = []
        first = 0
        for c, chunk in enumerate(Q_CHUNKS):
            raw = keep.tile([P, PACK, chunk], F32, name="query_raw%d" % c)
            nc.sync.dma_start(raw[:], query_rows[:, :, first : first + chunk])
            query_raw.append((raw, slice(first // PACK, (first + chunk) // PACK)))
            first += chunk
            if c == 0:
                word_store = keep.tile([P, T], U32, name="word_store")
                nc.sync.dma_start(word_store[:].bitcast(I32), piece_words[0].rearrange("p n t -> p (n t)").bitcast(I32))

        identity = keep.tile([P, P], F32, name="identity")
        make_identity(nc, identity[:])
        key_scales = keep.tile([P, I], U8, name="key_scales", align_bytes=64)
        nc.vector.memset(key_scales[:].bitcast(I32), 0)

        picked_scales = keep.tile([P, I], U8, name="picked_scales")
        nc.vector.tensor_copy(picked_scales[:], scale_store[:].indirect(piece_list[:]))
        for quad in range(4):
            nc.sync.dma_start(
                key_scales[32 * quad : 32 * quad + 4, :].bitcast(I32),
                picked_scales[32 * quad : 32 * quad + 32 : BLOCK_PARTS, :].bitcast(I32),
            )
        prior_rows = prior.rearrange("(p r) u -> p r u", r=PACK)
        prior_table = keep.tile([P, PACK, U], F32, name="prior_table", tag="scales_then_prior")
        for r in range(PACK):
            nc.sync.dma_start(prior_table[:, r, :], prior_rows[:, r, :])

        key_words = []
        for h in range(HALVES):
            picked = keep.tile([P, HALF], U32, name="key_words%d" % h, align_bytes=64)
            nc.vector.tensor_copy(picked[:], word_store[:].indirect(piece_list[:, h * HALF // 16 : (h + 1) * HALF // 16]))
            key_words.append(picked)

        query_bf = keep.tile([P, PACK, P, PACK], BF16, name="query_bf", align_bytes=64)
        for raw, ms in query_raw:
            nc.scalar.activation(
                query_bf[:, :, ms, :].rearrange("p r m t -> p m r t"),
                raw[:].rearrange("p t (m r) -> p m r t", r=PACK),
                ACT.Copy,
            )
        query_words, query_scales = [], []
        for r in range(PACK):
            query_words.append(keep.tile([P, P], U32, name="query_words%d" % r, align_bytes=64))
            query_scales.append(keep.tile([P, P], U8, name="query_scales%d" % r, align_bytes=64))
            nc.vector.quantize_mx(
                out=query_words[r][:].bitcast(FP8X4),
                scales=query_scales[r][:],
                in_=query_bf[:, r, :, :].rearrange("p m t -> p (m t)"),
            )

        last = PACK - 1
        picked_prior = keep.tile([P, PACK, G], F32, name="picked_prior")
        for r in range(last):
            nc.scalar.activation(picked_prior[:, r, :], prior_table[:, r, :].indirect(page_list[:]), ACT.Copy)
        neg_prior_max = keep.tile([P, PACK], F32, name="neg_prior_max")

        y = keep.tile([P, PACK, G], F32, name="y")
        slot_exps, neg_maxes = [], []
        for r in range(PACK):
            neg_max = keep.tile([P, HALVES], F32, name="neg_max%d" % r)
            slot_exp = keep.tile([P, I], F32, name="slot_exp%d" % r)
            for h in range(HALVES):
                scores = score_banks.tile([P, HALF], F32, name="scores", tag="scores")
                nc.tensor.matmul_mx(
                    out=scores[:],
                    lhsT=query_words[r][:].bitcast(FP8X4),
                    lhsT_scale=query_scales[r][:],
                    rhs=key_words[h][:].bitcast(FP8X4),
                    rhs_scale=key_scales[:, h * HALF : (h + 1) * HALF],
                    start=True,
                    stop=True,
                )
                nc.vector.tensor_reduce(neg_max[:, h : h + 1], scores[:], X, ALU.max, negate=True)
                pages = slice(h * HALF_PAGES, (h + 1) * HALF_PAGES)
                if r == last:
                    nc.scalar.activation(
                        slot_exp[:, h * HALF : (h + 1) * HALF], scores[:], ACT.Exp, bias=neg_max[:, h : h + 1]
                    )
                else:
                    nc.scalar.activation(
                        slot_exp[:].rearrange("p (k e g) -> p k g e", e=2, g=G)[:, :, pages, :],
                        scores[:].rearrange("p (g k e) -> p k g e", e=2, k=PAGE // 2),
                        ACT.Exp,
                        bias=neg_max[:, h : h + 1],
                    )
            slot_exps.append(slot_exp)
            neg_maxes.append(neg_max)
            if r == 1:
                nc.vector.tensor_copy(picked_prior[:, last, :], prior_table[:, last, :].indirect(page_list[:]))
            if r < 2:
                nc.vector.tensor_reduce(neg_prior_max[:, PAIRS[r]], picked_prior[:, PAIRS[r], :], X, ALU.max, negate=True)

        for r in range(PACK):
            slot_exp, neg_max = slot_exps[r], neg_maxes[r]
            small = nc.vector if r == last else nc.gpsimd
            neg_shift = keep.tile([P, 1], F32, name="neg_shift%d" % r)
            small.tensor_scalar(neg_shift[:], neg_max[:, 0:1], neg_max[:, 1:2], neg_prior_max[:, r : r + 1], ALU.min, ALU.add)
            page_bias = keep.tile([P, HALVES], F32, name="page_bias%d" % r)
            small.tensor_scalar(page_bias[:], neg_max[:], -1.0, neg_shift[:], ALU.mult, ALU.add)
            page_weight = keep.tile([P, G], F32, name="page_weight%d" % r)
            for h in range(HALVES):
                pages = slice(h * HALF_PAGES, (h + 1) * HALF_PAGES)
                nc.scalar.activation(page_weight[:, pages], picked_prior[:, r, pages], ACT.Exp, bias=page_bias[:, h : h + 1])
            if r == last:
                page_sum = keep.tile([P, G], F32, name="page_sum")
                for h in range(HALVES):
                    pages = slice(h * HALF_PAGES, (h + 1) * HALF_PAGES)
                    nc.vector.tensor_reduce(
                        page_sum[:, pages],
                        slot_exp[:, h * HALF : (h + 1) * HALF].rearrange("p (g j) -> p g j", j=PAGE),
                        X,
                        ALU.add,
                    )
            else:
                turned_sum = turn_banks.tile([P, P], F32, name="turned_sum")
                for j in range(PAGE):
                    nc.tensor.matmul(
                        turned_sum[:],
                        lhsT=slot_exp[:, j * G : (j + 1) * G],
                        rhs=identity[:],
                        start=(j == 0),
                        stop=(j == PAGE - 1),
                        is_transpose=True,
                    )
                turned_copy = keep.tile([P, P], F32, name="turned_copy%d" % r, align_bytes=64, tag="turned_copy%d" % r)
                nc.scalar.copy(turned_copy[:], turned_sum[:])
                page_sum = score_banks.tile([P, G], F32, name="page_sum_bank", tag="scores")
                nc.tensor.transpose(page_sum[:], turned_copy[:], identity[:])

            weighted = keep.tile([P, G], F32, name="weighted%d" % r)
            row_sum = keep.tile([P, 1], F32, name="row_sum%d" % r)
            nc.vector.scalar_tensor_tensor(
                weighted[:], page_sum[:], 1.0, page_weight[:], ALU.mult, ALU.mult, accum_out=row_sum[:]
            )
            inverse = keep.tile([P, 1], F32, name="inverse%d" % r)
            nc.vector.reciprocal(inverse[:], row_sum[:])
            if r == 2:
                y_bf = keep.tile([P, G, PACK], BF16, name="y_bf", align_bytes=64, tag="turned_copy2")
                nc.scalar.activation(y_bf[:, :, PAIRS[0]], y[:, PAIRS[0], :].rearrange("p r g -> p g r"), ACT.Copy)
            if r >= 2:
                nc.vector.tensor_scalar(y_bf[:, :, r], weighted[:], inverse[:], 64.0, ALU.mult, ALU.mult)
            scaler = nc.vector if r >= 2 else nc.gpsimd
            scaler.tensor_scalar(y[:, r, :], weighted[:], inverse[:], 64.0, ALU.mult, ALU.mult)
            if r % 2 == 1:
                pair = PAIRS[r // 2]
                nc.sync.dma_start(out_0.rearrange("(p r) g -> p r g", r=PACK)[:, pair, :], y[:, pair, :])

        y_words = keep.tile([P, G], U32, name="y_words", align_bytes=64)
        y_scales = keep.tile([P, G], U8, name="y_scales", align_bytes=64)
        nc.vector.quantize_mx(out=y_words[:].bitcast(FP8X4), scales=y_scales[:], in_=y_bf[:].rearrange("p g r -> p (g r)"))
        nc.sync.dma_start(out_1[0].rearrange("p g r -> p (g r)").bitcast(I32), y_words[:].bitcast(I32))
        for quad in range(4):
            queue = nc.scalar if quad % 2 == 0 else nc.sync
            queue.dma_start(
                out_2[0, 4 * quad : 4 * quad + 4, :].bitcast(I32),
                y_scales[32 * quad : 32 * quad + 4, :].bitcast(I32),
            )
